import numpy as np
import ml_dtypes


def mxq(x, axis, fmt="e4m3"):
    dtype, down = {"e4m3": (ml_dtypes.float8_e4m3fn, 7), "e5m2": (ml_dtypes.float8_e5m2, 14)}[fmt]
    v = np.moveaxis(np.asarray(x, np.float32).astype(ml_dtypes.bfloat16).astype(np.float64), axis, -1)
    blocks = v.reshape(v.shape[:-1] + (-1, 32))
    amax = np.abs(blocks).max(-1, keepdims=True)
    byte = np.maximum(np.where(amax > 0, np.frexp(amax)[1] - 1 + 127, 0) - down, 1)
    scale = np.exp2(byte - 127.0)
    codes = (blocks / scale).astype(np.float32).astype(dtype).astype(np.float64)
    return np.moveaxis((codes * scale).reshape(v.shape), -1, axis)


WIDE = False


def mx_kscale(k):
    if not WIDE:
        return np.ones(k)
    levels = np.array([10, -10, 5, -5, 0])
    if k % 512:
        return np.exp2(np.random.permutation(np.resize(levels, k // 32))).repeat(32)
    a = np.empty((k // 512, 16))
    for p in range(k // 512):
        a[p, :8] = np.random.permutation(np.resize(levels, 8))
        for g in range(8):
            far = levels[np.abs(levels - a[p, g]) >= 10]
            a[p, g + 8] = far[np.random.randint(len(far))]
    return np.exp2(a.ravel()).repeat(32)


def f64(x):
    return np.asarray(x).astype(np.float64)


def striped(idx):
    return np.tile(idx.reshape(-1, 16).T, (8, 1)).astype(np.uint16)


def unstriped(offs):
    return offs[:16].T.reshape(-1).astype(np.int64)


E2M1 = np.array([0.0, 0.5, 1.0, 1.5, 2.0, 3.0, 4.0, 6.0, -0.0, -0.5, -1.0, -1.5, -2.0, -3.0, -4.0, -6.0])


def pack_weight(w, fmt):
    k, n = w.shape
    w = f64(np.asarray(w, np.float32).astype(ml_dtypes.bfloat16)).reshape(k // 32, 32, n)
    amax = np.abs(w).max(1)
    if fmt == "e4m3":
        byte = np.frexp(amax)[1] - 1 + 127 - 7
    else:
        mant, ex = np.frexp(amax / 6.0)
        byte = np.where(mant > 0.5, ex, ex - 1) + 127
    byte = np.clip(np.where(amax > 0, byte, 1), 1, 254)
    scaled = (w * np.exp2(127.0 - byte)[:, None, :]).reshape(k, n).astype(np.float32)
    by_word = np.ascontiguousarray(scaled.reshape(k // 512, 128, 4, n).transpose(0, 1, 3, 2))
    if fmt == "e4m3":
        words = by_word.astype(ml_dtypes.float8_e4m3fn).view(np.uint8)
    else:
        c = by_word.astype(ml_dtypes.float4_e2m1fn).view(np.uint8) & 0xF
        words = (c[..., 0::2] | (c[..., 1::2] << 4)).reshape(k // 512, 128, 2 * n)
    return np.ascontiguousarray(words), np.ascontiguousarray(byte.astype(np.uint8).reshape(k // 512, 16, n))


def unpack_weight(words, scales, fmt):
    g, _, n = scales.shape
    words = np.ascontiguousarray(words).reshape(g, 128, n, -1)
    if fmt == "e4m3":
        vals = words.view(ml_dtypes.float8_e4m3fn).astype(np.float64)
    else:
        nib = np.empty((g, 128, n, 4), np.uint8)
        nib[..., 0::2] = words & 0xF
        nib[..., 1::2] = words >> 4
        vals = E2M1[nib]
    vals = vals * np.repeat(np.exp2(scales.astype(np.float64) - 127.0), 8, axis=1)[..., None]
    return vals.transpose(0, 1, 3, 2).reshape(g * 512, n)


K, T, E, C, N, TOP = 1024, 512, 12, 128, 256, 3


def by_expert(wq, xq):
    return np.concatenate([wq[e].T @ xq[:, e * C:(e + 1) * C] for e in range(E)], axis=1)


def setup_inputs():
    n = np.random.standard_normal
    s = mx_kscale(K)
    deal = np.repeat(np.arange(E), C).reshape(TOP, T)[:, np.random.permutation(T)]
    deal = np.take_along_axis(deal, np.argsort(np.random.rand(TOP, T), axis=0), axis=0)
    for _ in range(8):
        s_, t_ = np.random.permutation(T).reshape(2, -1); r = np.random.randint(TOP, size=T // 2); x, y = deal[r, s_].copy(), deal[r, t_].copy()
        ok = ~((deal[:, s_] == y).any(0) | (deal[:, t_] == x).any(0)); deal[r[ok], s_[ok]] = y[ok]; deal[r[ok], t_[ok]] = x[ok]
    order = np.lexsort((np.random.rand(TOP * T), deal.reshape(-1)))
    slot_token = order % T; pos = np.empty(TOP * T, np.int64); pos[order] = np.arange(TOP * T); pos = pos.reshape(TOP, T)
    g = np.random.uniform(0.5, 1.5, (TOP, T)); g = g / g.sum(0)
    x = pack_weight(n((K, T)) * s[:, None], "e4m3")
    wq = [pack_weight(m, "e2m1") for m in n((E, K, N)) / np.sqrt(K) / s[None, :, None]]
    wv = [pack_weight(m, "e2m1") for m in n((E, K, N)) / np.sqrt(K) / s[None, :, None]]
    return {
        "x_words": x[0],
        "x_scales": x[1],
        "wq_words": np.stack([m[0] for m in wq]),
        "wq_scales": np.stack([m[1] for m in wq]),
        "wk": (n((E, K, N)) / np.sqrt(K) / s[None, :, None]).astype(np.float32),
        "wv_words": np.stack([m[0] for m in wv]),
        "wv_scales": np.stack([m[1] for m in wv]),
        "bias": (0.3 * n((3 * N, E))).astype(np.float32),
        "gate": np.stack([np.tile(r, (128, 1)) for r in g]).astype(np.float32),
        "offs": striped(slot_token),
        "pos1": striped(pos[0]),
        "pos2": striped(pos[1]),
        "pos3": striped(pos[2]),
    }


def reference(x_words, x_scales, wq_words, wq_scales, wk, wv_words, wv_scales, bias, gate, offs, pos1, pos2, pos3):
    wq = np.stack([unpack_weight(wq_words[e], wq_scales[e], "e2m1") for e in range(E)])
    wkq = mxq(f64(wk), 1, "e4m3")
    wv = np.stack([unpack_weight(wv_words[e], wv_scales[e], "e2m1") for e in range(E)])
    idx = unstriped(offs)
    xq = unpack_weight(x_words, x_scales, "e4m3")[:, idx]
    y = np.concatenate([by_expert(w, xq) for w in (wq, wkq, wv)])
    y = y + np.repeat(f64(bias), C, axis=1)
    out = sum(f64(gate[r, :1]) * y[:, unstriped(p)] for r, p in enumerate((pos1, pos2, pos3)))
    return out

@@ -1,0 +1,323 @@
+from contextlib import ExitStack
+
+import concourse.mybir as mybir
+
+K, T, E, C, N, TOP = 1024, 512, 12, 128, 256, 3
+FLOPS = 2 * E * C * K * 3 * N
+
+F32 = mybir.dt.float32
+BF16 = mybir.dt.bfloat16
+I32 = mybir.dt.int32
+U32 = mybir.dt.uint32
+U16 = mybir.dt.uint16
+U8 = mybir.dt.uint8
+FP8X4 = mybir.dt.float8_e4m3fn_x4
+FP4X4 = mybir.dt.float4_e2m1fn_x4
+MULT = mybir.AluOpType.mult
+ADD = mybir.AluOpType.add
+IDENTITY = mybir.ActivationFunctionType.Identity
+
+P = 128
+PACK = 4
+PASSES = K // (P * PACK)
+S = E * C
+HALVES = N // P
+CHUNK = 3
+LIST_ROWS = 16
+SLOTS = 19
+
+
+def tile_moe_qkv_kernel(
+    tc, x_words, x_scales, wq_words, wq_scales, wk, wv_words, wv_scales, bias, gate, offs, pos1, pos2, pos3, out
+):
+    nc = tc.nc
+    with ExitStack() as ctx:
+        keep = ctx.enter_context(tc.tile_pool(name="keep", bufs=1))
+        raw_pool = ctx.enter_context(tc.tile_pool(name="raw", bufs=20))
+        ring = ctx.enter_context(tc.tile_pool(name="ring", bufs=6))
+        psum = ctx.enter_context(tc.psum_pool(name="psum", bufs=8))
+
+        offs_t = keep.tile([P, S // LIST_ROWS], U16, name="offs_t")
+        pos_t = [keep.tile([P, T // LIST_ROWS], U16, name=f"pos{r}_t") for r in range(TOP)]
+        xw = [keep.tile([P, T], I32, name=f"xw{s}", align_bytes=64) for s in range(PASSES)]
+        xs = keep.tile([P, T], U8, name="xs", align_bytes=64)
+        slot_words = keep.tile([P, PASSES, S], U32, name="slot_words", align_bytes=64)
+        slot_scales = [keep.tile([P, S], U8, name=f"slot_scales{s}", align_bytes=64) for s in range(PASSES)]
+        packed_words = [keep.tile([P, E * PASSES, 2 * N], U8, name=f"packed_words{i}", align_bytes=64) for i in range(2)]
+        packed_scales = [keep.tile([P, E * PASSES, N], U8, name=f"packed_scales{i}", align_bytes=64) for i in range(2)]
+        bias_t = keep.tile([P, 3 * HALVES, 16], F32, name="bias_t")
+        gate_t = keep.tile([P, TOP, T], F32, name="gate_t")
+        y = [keep.tile([P, S], F32, name=f"y{j}") for j in range(3 * HALVES)]
+        work = keep.tile([P, SLOTS, T], F32, name="work", align_bytes=64)
+
+        nc.vector.memset(xs[:].bitcast(I32), 0)
+        nc.vector.memset(packed_scales[0][:].rearrange("p a n -> p (a n)").bitcast(I32), 0)
+        nc.vector.memset(slot_scales[1][:].bitcast(I32), 0)
+        nc.vector.memset(packed_scales[1][:].rearrange("p a n -> p (a n)").bitcast(I32), 0)
+
+        raw = {}
+
+        def load_wk(e):
+            for s in range(PASSES):
+                raw[e, s] = raw_pool.tile([P, PACK, N], F32, name="raw")
+                rows = wk[e, s * P * PACK : (s + 1) * P * PACK, :]
+                nc.sync.dma_start(out=raw[e, s][:], in_=rows.rearrange("(p d) n -> p d n", d=PACK))
+
+        def load_packed_words(i, words, e0, e1):
+            nc.sync.dma_start(
+                out=packed_words[i][:, e0 * PASSES : e1 * PASSES, :].bitcast(I32),
+                in_=words[e0:e1].rearrange("e s p b -> p (e s) b").bitcast(I32),
+            )
+
+        def load_packed_scales(i, scales):
+            for r in range(4):
+                nc.sync.dma_start(
+                    out=packed_scales[i][r:P:32, :, :].bitcast(I32),
+                    in_=scales[:, :, r:16:4, :].rearrange("e s q n -> q (e s) n").bitcast(I32),
+                )
+
+        def load_x_words(s):
+            nc.sync.dma_start(out=xw[s][:], in_=x_words[s].rearrange("p t d -> p (t d)").bitcast(I32))
+
+        nc.sync.dma_start(offs_t[:], offs)
+        for q in range(4):
+            nc.sync.dma_start(
+                out=xs[32 * q : 32 * q + 4 * PASSES, :].bitcast(I32),
+                in_=x_scales[:, 4 * q : 4 * q + 4, :].bitcast(I32),
+            )
+        load_x_words(0)
+        load_x_words(1)
+        load_wk(0)
+        nc.sync.dma_start(out=bias_t[:, :, :E], in_=bias.rearrange("(j p) e -> p j e", p=P))
+        load_wk(1)
+        load_packed_scales(0, wq_scales)
+        load_packed_words(0, wq_words, 0, E // 2)
+        load_packed_words(0, wq_words, E // 2, E)
+        for r, src in enumerate((pos1, pos2, pos3)):
+            nc.sync.dma_start(pos_t[r][:], src)
+            nc.sync.dma_start(out=gate_t[:, r, :], in_=gate[r])
+        load_wk(2)
+        load_packed_scales(1, wv_scales)
+        load_packed_words(1, wv_words, 0, E // 2)
+        load_packed_words(1, wv_words, E // 2, E)
+        for e in range(3, E):
+            load_wk(e)
+
+        def chunk(c):
+            slots = slice(c * CHUNK * C, (c + 1) * CHUNK * C)
+            return slots, offs_t[:, slots.start // LIST_ROWS : slots.stop // LIST_ROWS]
+
+        def gather_scales():
+            for c in range(E // CHUNK):
+                slots, entries = chunk(c)
+                nc.vector.tensor_copy(slot_scales[0][:, slots], xs[:].indirect(entries))
+
+        def move_scales():
+            nc.gpsimd.dma_start(out=slot_scales[1][0:112, :].bitcast(I32), in_=slot_scales[0][4:116, :].bitcast(I32))
+
+        def gather_words(c):
+            slots, entries = chunk(c)
+            for s in range(PASSES):
+                nc.vector.tensor_copy(slot_words[:, s, slots], xw[s][:].bitcast(U32).indirect(entries))
+
+        sums = {}
+
+        def multiply(first_tile, e, h, operand, token_scales):
+            slots = slice(e * C, (e + 1) * C)
+            sums[first_tile + h, e] = psum.tile([P, C], F32, name="acc")
+            for s in range(PASSES):
+                codes, scales = operand(s, h)
+                nc.tensor.matmul_mx(
+                    out=sums[first_tile + h, e][:],
+                    lhsT=codes,
+                    lhsT_scale=scales,
+                    rhs=slot_words[:, s, slots].bitcast(FP8X4),
+                    rhs_scale=token_scales[s][:, slots],
+                    start=(s == 0),
+                    stop=(s == PASSES - 1),
+                )
+
+        def add_bias(j, e):
+            nc.scalar.activation(
+                out=y[j][:, e * C : (e + 1) * C], in_=sums[j, e][:], func=IDENTITY, bias=bias_t[:, j, e : e + 1]
+            )
+
+        def project_packed(i, e, halves):
+            def operand(s, h):
+                a = e * PASSES + s
+                return (
+                    packed_words[i][:, a, 2 * P * h : 2 * P * (h + 1)].bitcast(FP4X4),
+                    packed_scales[i][:, a, P * h : P * (h + 1)],
+                )
+
+            for h in halves:
+                multiply(2 * HALVES * i, e, h, operand, slot_scales)
+                add_bias(2 * HALVES * i + h, e)
+
+        def project_all_packed(i):
+            for e in range(E // 2):
+                project_packed(i, e, range(HALVES))
+            for h in range(HALVES):
+                for e in range(E // 2, E):
+                    project_packed(i, e, [h])
+
+        slot_of = {}
+        fresh = list(range(SLOTS))
+
+        def interleave(engine, e, s, after=None, halves=slice(0, HALVES)):
+            if (e, s) not in slot_of:
+                slot_of[e, s] = fresh.pop(0) if after is None else slot_of[after]
+            dst = work[:, slot_of[e, s], :].bitcast(BF16).rearrange("p (c i d) -> p c d i", i=4, d=PACK)
+            src = raw[e, s][:].rearrange("p d (c i) -> p c d i", i=4)
+            cols = slice(halves.start * P // 4, halves.stop * P // 4)
+            if engine == "vector":
+                nc.vector.tensor_copy(out=dst[:, cols], in_=src[:, cols])
+            else:
+                nc.scalar.copy(out=dst[:, cols], in_=src[:, cols])
+
+        quantised = {}
+
+        def quantise(e, s, halves=slice(0, HALVES)):
+            if (e, s) not in quantised:
+                codes = ring.tile([P, N], U32, name="key_codes", align_bytes=64)
+                scales = ring.tile([P, N], U8, name="key_scales", align_bytes=64)
+                quantised[e, s] = (codes, scales)
+            codes, scales = quantised[e, s]
+            cols = slice(halves.start * P, halves.stop * P)
+            grouped = work[:, slot_of[e, s], :].bitcast(BF16)
+            nc.vector.quantize_mx(
+                out=codes[:, cols].bitcast(FP8X4), scales=scales[:, cols], in_=grouped[:, cols.start * PACK : cols.stop * PACK]
+            )
+
+        def multiply_keys(e, halves=range(HALVES)):
+            def operand(s, h):
+                codes, scales = quantised[e, s]
+                return codes[:, P * h : P * (h + 1)].bitcast(FP8X4), scales[:, P * h : P * (h + 1)]
+
+            for h in halves:
+                multiply(HALVES, e, h, operand, [slot_scales[0][:, :], slot_scales[0][4:P, :]])
+
+        def bias_keys(e, halves=range(HALVES)):
+            for h in halves:
+                add_bias(HALVES + h, e)
+
+        def fetch(j, r, after, cols=slice(0, T)):
+            slot_of["product", j, r] = slot_of[after]
+            entries = pos_t[r][:, cols.start // LIST_ROWS : cols.stop // LIST_ROWS]
+            nc.vector.tensor_tensor(work[:, slot_of[after], cols], y[j][:].indirect(entries), gate_t[:, r, cols], MULT)
+
+        def accumulate(j, r, cols=slice(0, T)):
+            total = work[:, slot_of["product", j, 0], cols]
+            nc.vector.tensor_tensor(total, total, work[:, slot_of["product", j, r], cols], ADD)
+            if r == TOP - 1:
+                nc.sync.dma_start(out=out[j * P : (j + 1) * P, cols], in_=total)
+
+        def scalar_expert(e):
+            for s in range(PASSES):
+                interleave("scalar", e, s)
+
+        scalar_expert(0)
+        gather_words(0)
+        gather_scales()
+        move_scales()
+        scalar_expert(1)
+        gather_words(1)
+        quantise(0, 0)
+        quantise(0, 1)
+        multiply_keys(0)
+        gather_words(2)
+        quantise(1, 0)
+        quantise(1, 1)
+        multiply_keys(1)
+        gather_words(3)
+        bias_keys(0)
+        bias_keys(1)
+        project_all_packed(0)
+        scalar_expert(2)
+        fetch(0, 0, (0, 0))
+        fetch(0, 1, (0, 1))
+        fetch(0, 2, (1, 0))
+        quantise(2, 0)
+        accumulate(0, 1)
+        quantise(2, 1)
+        multiply_keys(2)
+        accumulate(0, 2)
+        bias_keys(2)
+        project_all_packed(1)
+        scalar_expert(3)
+        fetch(1, 0, (2, 1))
+        fetch(1, 1, (2, 0))
+        fetch(1, 2, (1, 1))
+        accumulate(1, 1)
+        fetch(4, 0, ("product", 0, 1))
+        accumulate(1, 2)
+        fetch(4, 1, ("product", 0, 2))
+        scalar_expert(4)
+        quantise(3, 0)
+        fetch(4, 2, (3, 0))
+        quantise(3, 1)
+        multiply_keys(3)
+        accumulate(4, 1)
+        quantise(4, 0)
+        accumulate(4, 2)
+        bias_keys(3)
+        scalar_expert(5)
+        fetch(5, 0, (4, 0))
+        quantise(4, 1)
+        multiply_keys(4)
+        fetch(5, 1, (4, 1))
+        quantise(5, 0)
+        bias_keys(4)
+        scalar_expert(6)
+        fetch(5, 2, (5, 0))
+        quantise(5, 1)
+        multiply_keys(5)
+        accumulate(5, 1)
+        quantise(6, 0)
+        accumulate(5, 2)
+        bias_keys(5)
+        scalar_expert(7)
+        quantise(6, 1)
+        multiply_keys(6)
+        interleave("vector", 8, 0, ("product", 5, 1))
+        quantise(7, 0)
+        bias_keys(6)
+        interleave("vector", 8, 1, ("product", 5, 2))
+        quantise(8, 0)
+        quantise(7, 1)
+        multiply_keys(7)
+        quantise(8, 1)
+        multiply_keys(8)
+        for e in (9, 10):
+            interleave("scalar", e, 0)
+            interleave("vector", e, 1, (e - 1, 1))
+            bias_keys(e - 2)
+            quantise(e, 0)
+            quantise(e, 1)
+            multiply_keys(e)
+        interleave("scalar", 11, 0)
+        bias_keys(9)
+        interleave("vector", 11, 1, (10, 1), slice(0, 1))
+        interleave("scalar", 11, 1, (10, 1), slice(1, 2))
+        quantise(11, 0)
+        quantise(11, 1, slice(0, 1))
+        multiply_keys(11, [0])
+        quantise(11, 1, slice(1, 2))
+        multiply_keys(11, [1])
+        bias_keys(10, [0])
+        bias_keys(11, [0])
+        bias_keys(10, [1])
+        bias_keys(11, [1])
+        fetch(2, 0, (5, 1))
+        fetch(2, 1, (6, 0))
+        fetch(2, 2, (6, 1))
+        accumulate(2, 1)
+        fetch(3, 0, (7, 0))
+        accumulate(2, 2)
+        fetch(3, 1, (7, 1))
+        token_halves = [slice(0, T // 2), slice(T // 2, T)]
+        fetch(3, 2, (9, 0), token_halves[0])
+        accumulate(3, 1)
+        fetch(3, 2, (9, 0), token_halves[1])
+        accumulate(3, 2, token_halves[0])
+        accumulate(3, 2, token_halves[1])

@@ -34,8 +34,8 @@ def tile_moe_qkv_kernel(
     with ExitStack() as ctx:
         keep = ctx.enter_context(tc.tile_pool(name="keep", bufs=1))
         raw_pool = ctx.enter_context(tc.tile_pool(name="raw", bufs=20))
-        ring = ctx.enter_context(tc.tile_pool(name="ring", bufs=6))
-        psum = ctx.enter_context(tc.psum_pool(name="psum", bufs=8))
+        ring = ctx.enter_context(tc.tile_pool(name="ring", bufs=8))
+        psum = ctx.enter_context(tc.psum_pool(name="psum", bufs=1))
 
         offs_t = keep.tile([P, S // LIST_ROWS], U16, name="offs_t")
         pos_t = [keep.tile([P, T // LIST_ROWS], U16, name=f"pos{r}_t") for r in range(TOP)]
@@ -57,11 +57,10 @@ def tile_moe_qkv_kernel(
 
         raw = {}
 
-        def load_wk(e):
-            for s in range(PASSES):
-                raw[e, s] = raw_pool.tile([P, PACK, N], F32, name="raw")
-                rows = wk[e, s * P * PACK : (s + 1) * P * PACK, :]
-                nc.sync.dma_start(out=raw[e, s][:], in_=rows.rearrange("(p d) n -> p d n", d=PACK))
+        def load_wk(e, s):
+            raw[e, s] = raw_pool.tile([P, PACK, N], F32, name="raw")
+            rows = wk[e, s * P * PACK : (s + 1) * P * PACK, :]
+            nc.sync.dma_start(out=raw[e, s][:], in_=rows.rearrange("(p d) n -> p d n", d=PACK))
 
         def load_packed_words(i, words, e0, e1):
             nc.sync.dma_start(
@@ -87,21 +86,47 @@ def tile_moe_qkv_kernel(
             )
         load_x_words(0)
         load_x_words(1)
-        load_wk(0)
+        load_wk(0, 0)
+        load_wk(0, 1)
         nc.sync.dma_start(out=bias_t[:, :, :E], in_=bias.rearrange("(j p) e -> p j e", p=P))
-        load_wk(1)
+        load_wk(1, 0)
+        load_wk(1, 1)
         load_packed_scales(0, wq_scales)
-        load_packed_words(0, wq_words, 0, E // 2)
-        load_packed_words(0, wq_words, E // 2, E)
-        for r, src in enumerate((pos1, pos2, pos3)):
-            nc.sync.dma_start(pos_t[r][:], src)
-            nc.sync.dma_start(out=gate_t[:, r, :], in_=gate[r])
-        load_wk(2)
+        load_packed_words(0, wq_words, 0, 3)
+        load_packed_words(0, wq_words, 3, 6)
+        load_packed_words(0, wq_words, 6, 9)
+        load_packed_words(0, wq_words, 9, 12)
+        nc.sync.dma_start(pos_t[0][:], pos1)
+        nc.sync.dma_start(out=gate_t[:, 0, :], in_=gate[0])
+        nc.sync.dma_start(pos_t[1][:], pos2)
+        nc.sync.dma_start(out=gate_t[:, 1, :], in_=gate[1])
+        nc.sync.dma_start(pos_t[2][:], pos3)
+        nc.sync.dma_start(out=gate_t[:, 2, :], in_=gate[2])
+        load_wk(2, 0)
+        load_wk(2, 1)
         load_packed_scales(1, wv_scales)
-        load_packed_words(1, wv_words, 0, E // 2)
-        load_packed_words(1, wv_words, E // 2, E)
-        for e in range(3, E):
-            load_wk(e)
+        load_packed_words(1, wv_words, 0, 3)
+        load_packed_words(1, wv_words, 3, 6)
+        load_packed_words(1, wv_words, 6, 9)
+        load_packed_words(1, wv_words, 9, 12)
+        load_wk(3, 0)
+        load_wk(3, 1)
+        load_wk(4, 0)
+        load_wk(4, 1)
+        load_wk(5, 0)
+        load_wk(5, 1)
+        load_wk(6, 0)
+        load_wk(6, 1)
+        load_wk(7, 0)
+        load_wk(7, 1)
+        load_wk(8, 0)
+        load_wk(8, 1)
+        load_wk(9, 0)
+        load_wk(9, 1)
+        load_wk(10, 0)
+        load_wk(10, 1)
+        load_wk(11, 0)
+        load_wk(11, 1)
 
         def chunk(c):
             slots = slice(c * CHUNK * C, (c + 1) * CHUNK * C)
@@ -120,11 +145,12 @@ def tile_moe_qkv_kernel(
             for s in range(PASSES):
                 nc.vector.tensor_copy(slot_words[:, s, slots], xw[s][:].bitcast(U32).indirect(entries))
 
+        banks = [psum.tile([P, C], F32, name=f"bank{b}") for b in range(8)]
         sums = {}
 
         def multiply(first_tile, e, h, operand, token_scales):
             slots = slice(e * C, (e + 1) * C)
-            sums[first_tile + h, e] = psum.tile([P, C], F32, name="acc")
+            sums[first_tile + h, e] = banks[len(sums) % len(banks)]
             for s in range(PASSES):
                 codes, scales = operand(s, h)
                 nc.tensor.matmul_mx(
@@ -155,10 +181,10 @@ def tile_moe_qkv_kernel(
                 add_bias(2 * HALVES * i + h, e)
 
         def project_all_packed(i):
-            for e in range(E // 2):
+            for e in range(9):
                 project_packed(i, e, range(HALVES))
             for h in range(HALVES):
-                for e in range(E // 2, E):
+                for e in range(9, E):
                     project_packed(i, e, [h])
 
         slot_of = {}
@@ -217,42 +243,42 @@ def tile_moe_qkv_kernel(
                 interleave("scalar", e, s)
 
         scalar_expert(0)
-        gather_words(0)
         gather_scales()
         move_scales()
+        gather_words(0)
         scalar_expert(1)
         gather_words(1)
+        gather_words(2)
+        gather_words(3)
         quantise(0, 0)
         quantise(0, 1)
-        multiply_keys(0)
-        gather_words(2)
         quantise(1, 0)
         quantise(1, 1)
-        multiply_keys(1)
-        gather_words(3)
-        bias_keys(0)
-        bias_keys(1)
         project_all_packed(0)
         scalar_expert(2)
+        for e in (0, 1):
+            multiply_keys(e)
+            bias_keys(e)
         fetch(0, 0, (0, 0))
         fetch(0, 1, (0, 1))
         fetch(0, 2, (1, 0))
-        quantise(2, 0)
         accumulate(0, 1)
-        quantise(2, 1)
-        multiply_keys(2)
+        fetch(1, 0, (1, 1))
         accumulate(0, 2)
-        bias_keys(2)
+        fetch(1, 1, ("product", 0, 1))
+        quantise(2, 0)
+        fetch(1, 2, (2, 0))
+        quantise(2, 1)
+        accumulate(1, 1)
         project_all_packed(1)
         scalar_expert(3)
-        fetch(1, 0, (2, 1))
-        fetch(1, 1, (2, 0))
-        fetch(1, 2, (1, 1))
-        accumulate(1, 1)
-        fetch(4, 0, ("product", 0, 1))
+        multiply_keys(2)
+        fetch(4, 0, (2, 1))
         accumulate(1, 2)
         fetch(4, 1, ("product", 0, 2))
-        scalar_expert(4)
+        interleave("scalar", 4, 0)
+        bias_keys(2)
+        interleave("scalar", 4, 1)
         quantise(3, 0)
         fetch(4, 2, (3, 0))
         quantise(3, 1)
@@ -260,28 +286,27 @@ def tile_moe_qkv_kernel(
         accumulate(4, 1)
         quantise(4, 0)
         accumulate(4, 2)
-        bias_keys(3)
         scalar_expert(5)
+        bias_keys(3)
         fetch(5, 0, (4, 0))
         quantise(4, 1)
         multiply_keys(4)
         fetch(5, 1, (4, 1))
         quantise(5, 0)
-        bias_keys(4)
         scalar_expert(6)
+        bias_keys(4)
         fetch(5, 2, (5, 0))
         quantise(5, 1)
         multiply_keys(5)
         accumulate(5, 1)
         quantise(6, 0)
         accumulate(5, 2)
-        bias_keys(5)
         scalar_expert(7)
+        bias_keys(5)
         quantise(6, 1)
         multiply_keys(6)
         interleave("vector", 8, 0, ("product", 5, 1))
         quantise(7, 0)
-        bias_keys(6)
         interleave("vector", 8, 1, ("product", 5, 2))
         quantise(8, 0)
         quantise(7, 1)
@@ -291,10 +316,11 @@ def tile_moe_qkv_kernel(
         for e in (9, 10):
             interleave("scalar", e, 0)
             interleave("vector", e, 1, (e - 1, 1))
-            bias_keys(e - 2)
+            bias_keys(e - 3)
             quantise(e, 0)
             quantise(e, 1)
             multiply_keys(e)
+        bias_keys(8)
         interleave("scalar", 11, 0)
         bias_keys(9)
         interleave("vector", 11, 1, (10, 1), slice(0, 1))

@@ -24,7 +24,7 @@ S = E * C
 HALVES = N // P
 CHUNK = 3
 LIST_ROWS = 16
-SLOTS = 19
+SLOTS = 4
 
 
 def tile_moe_qkv_kernel(
@@ -43,8 +43,12 @@ def tile_moe_qkv_kernel(
         xs = keep.tile([P, T], U8, name="xs", align_bytes=64)
         slot_words = keep.tile([P, PASSES, S], U32, name="slot_words", align_bytes=64)
         slot_scales = [keep.tile([P, S], U8, name=f"slot_scales{s}", align_bytes=64) for s in range(PASSES)]
-        packed_words = [keep.tile([P, E * PASSES, 2 * N], U8, name=f"packed_words{i}", align_bytes=64) for i in range(2)]
-        packed_scales = [keep.tile([P, E * PASSES, N], U8, name=f"packed_scales{i}", align_bytes=64) for i in range(2)]
+        packed_words = [
+            keep.tile([P, E * PASSES, 2 * N], U8, name=f"packed_words{i}", tag=f"words{i}", align_bytes=64) for i in range(2)
+        ]
+        packed_scales = [
+            keep.tile([P, E * PASSES, N], U8, name=f"packed_scales{i}", tag=f"scales{i}", align_bytes=64) for i in range(2)
+        ]
         bias_t = keep.tile([P, 3 * HALVES, 16], F32, name="bias_t")
         gate_t = keep.tile([P, TOP, T], F32, name="gate_t")
         y = [keep.tile([P, S], F32, name=f"y{j}") for j in range(3 * HALVES)]
@@ -74,6 +78,17 @@ def tile_moe_qkv_kernel(
                     out=packed_scales[i][r:P:32, :, :].bitcast(I32),
                     in_=scales[:, :, r:16:4, :].rearrange("e s q n -> q (e s) n").bitcast(I32),
                 )
+
+        key_bias = {}
+
+        def load_key_bias(e0, e1):
+            later = keep.tile([P, HALVES, 8], F32, name=f"key_bias{e0}")
+            nc.sync.dma_start(
+                out=later[:, :, : e1 - e0], in_=bias[N : 2 * N, e0:e1].rearrange("(h p) e -> p h e", p=P)
+            )
+            for e in range(e0, e1):
+                for h in range(HALVES):
+                    key_bias[HALVES + h, e] = later[:, h, e - e0 : e - e0 + 1]
 
         def load_x_words(s):
             nc.sync.dma_start(out=xw[s][:], in_=x_words[s].rearrange("p t d -> p (t d)").bitcast(I32))
@@ -119,6 +134,7 @@ def tile_moe_qkv_kernel(
         load_wk(6, 1)
         load_wk(7, 0)
         load_wk(7, 1)
+        load_key_bias(3, 11)
         load_wk(8, 0)
         load_wk(8, 1)
         load_wk(9, 0)
@@ -150,7 +166,8 @@ def tile_moe_qkv_kernel(
 
         def multiply(first_tile, e, h, operand, token_scales):
             slots = slice(e * C, (e + 1) * C)
-            sums[first_tile + h, e] = banks[len(sums) % len(banks)]
+            banks.append(banks.pop(0))
+            sums[first_tile + h, e] = banks[-1]
             for s in range(PASSES):
                 codes, scales = operand(s, h)
                 nc.tensor.matmul_mx(
@@ -163,9 +180,13 @@ def tile_moe_qkv_kernel(
                     stop=(s == PASSES - 1),
                 )
 
+        def step_back(count):
+            for turn in range(count):
+                banks.insert(0, banks.pop())
+
         def add_bias(j, e):
             nc.scalar.activation(
-                out=y[j][:, e * C : (e + 1) * C], in_=sums[j, e][:], func=IDENTITY, bias=bias_t[:, j, e : e + 1]
+                out=y[j][:, e * C : (e + 1) * C], in_=sums[j, e][:], func=IDENTITY, bias=key_bias.get((j, e), bias_t[:, j, e : e + 1])
             )
 
         def project_packed(i, e, halves):
@@ -188,12 +209,16 @@ def tile_moe_qkv_kernel(
                     project_packed(i, e, [h])
 
         slot_of = {}
-        fresh = list(range(SLOTS))
+        fresh = [work[:, b, :] for b in range(SLOTS)]
+
+        def reuse(tag, count):
+            later = keep.tile([P, count, T], F32, name=f"after_{tag}", tag=tag, align_bytes=64)
+            return [later[:, b, :] for b in range(count)]
 
         def interleave(engine, e, s, after=None, halves=slice(0, HALVES)):
             if (e, s) not in slot_of:
                 slot_of[e, s] = fresh.pop(0) if after is None else slot_of[after]
-            dst = work[:, slot_of[e, s], :].bitcast(BF16).rearrange("p (c i d) -> p c d i", i=4, d=PACK)
+            dst = slot_of[e, s].bitcast(BF16).rearrange("p (c i d) -> p c d i", i=4, d=PACK)
             src = raw[e, s][:].rearrange("p d (c i) -> p c d i", i=4)
             cols = slice(halves.start * P // 4, halves.stop * P // 4)
             if engine == "vector":
@@ -210,7 +235,7 @@ def tile_moe_qkv_kernel(
                 quantised[e, s] = (codes, scales)
             codes, scales = quantised[e, s]
             cols = slice(halves.start * P, halves.stop * P)
-            grouped = work[:, slot_of[e, s], :].bitcast(BF16)
+            grouped = slot_of[e, s].bitcast(BF16)
             nc.vector.quantize_mx(
                 out=codes[:, cols].bitcast(FP8X4), scales=scales[:, cols], in_=grouped[:, cols.start * PACK : cols.stop * PACK]
             )
@@ -230,11 +255,11 @@ def tile_moe_qkv_kernel(
         def fetch(j, r, after, cols=slice(0, T)):
             slot_of["product", j, r] = slot_of[after]
             entries = pos_t[r][:, cols.start // LIST_ROWS : cols.stop // LIST_ROWS]
-            nc.vector.tensor_tensor(work[:, slot_of[after], cols], y[j][:].indirect(entries), gate_t[:, r, cols], MULT)
+            nc.vector.tensor_tensor(slot_of[after][:, cols], y[j][:].indirect(entries), gate_t[:, r, cols], MULT)
 
         def accumulate(j, r, cols=slice(0, T)):
-            total = work[:, slot_of["product", j, 0], cols]
-            nc.vector.tensor_tensor(total, total, work[:, slot_of["product", j, r], cols], ADD)
+            total = slot_of["product", j, 0][:, cols]
+            nc.vector.tensor_tensor(total, total, slot_of["product", j, r][:, cols], ADD)
             if r == TOP - 1:
                 nc.sync.dma_start(out=out[j * P : (j + 1) * P, cols], in_=total)
 
@@ -255,10 +280,15 @@ def tile_moe_qkv_kernel(
         quantise(1, 0)
         quantise(1, 1)
         project_all_packed(0)
-        scalar_expert(2)
+        step_back(4)
+        after_queries = reuse("words0", 6)
+        fresh.extend(after_queries[:2])
+        for b in range(4):
+            slot_of["spare", b] = after_queries[2 + b]
         for e in (0, 1):
             multiply_keys(e)
             bias_keys(e)
+        scalar_expert(2)
         fetch(0, 0, (0, 0))
         fetch(0, 1, (0, 1))
         fetch(0, 2, (1, 0))
@@ -271,6 +301,8 @@ def tile_moe_qkv_kernel(
         quantise(2, 1)
         accumulate(1, 1)
         project_all_packed(1)
+        step_back(2)
+        fresh.extend(reuse("words1", 6) + reuse("scales1", 3))
         scalar_expert(3)
         multiply_keys(2)
         fetch(4, 0, (2, 1))
@@ -279,71 +311,71 @@ def tile_moe_qkv_kernel(
         interleave("scalar", 4, 0)
         bias_keys(2)
         interleave("scalar", 4, 1)
+        fetch(4, 2, ("spare", 0))
+        accumulate(4, 1)
+        fetch(5, 0, ("spare", 1))
+        accumulate(4, 2)
+        fetch(5, 1, ("spare", 2))
+        fetch(5, 2, ("spare", 3))
+        accumulate(5, 1)
         quantise(3, 0)
-        fetch(4, 2, (3, 0))
+        accumulate(5, 2)
+        scalar_expert(5)
+        scalar_expert(6)
+        interleave("scalar", 7, 0)
+        interleave("scalar", 7, 1, ("product", 4, 1))
         quantise(3, 1)
         multiply_keys(3)
-        accumulate(4, 1)
-        quantise(4, 0)
-        accumulate(4, 2)
-        scalar_expert(5)
-        bias_keys(3)
-        fetch(5, 0, (4, 0))
-        quantise(4, 1)
-        multiply_keys(4)
-        fetch(5, 1, (4, 1))
-        quantise(5, 0)
-        scalar_expert(6)
-        bias_keys(4)
-        fetch(5, 2, (5, 0))
-        quantise(5, 1)
-        multiply_keys(5)
-        accumulate(5, 1)
-        quantise(6, 0)
-        accumulate(5, 2)
-        scalar_expert(7)
-        bias_keys(5)
-        quantise(6, 1)
-        multiply_keys(6)
-        interleave("vector", 8, 0, ("product", 5, 1))
-        quantise(7, 0)
-        interleave("vector", 8, 1, ("product", 5, 2))
-        quantise(8, 0)
-        quantise(7, 1)
-        multiply_keys(7)
-        quantise(8, 1)
-        multiply_keys(8)
-        for e in (9, 10):
-            interleave("scalar", e, 0)
-            interleave("vector", e, 1, (e - 1, 1))
-            bias_keys(e - 3)
+        for e in (4, 5, 6):
             quantise(e, 0)
             quantise(e, 1)
             multiply_keys(e)
+        interleave("vector", 8, 0, (6, 0))
+        quantise(7, 0)
+        interleave("vector", 8, 1, (7, 0))
+        bias_keys(3)
+        bias_keys(4)
+        quantise(7, 1)
+        multiply_keys(7)
+        quantise(8, 0)
+        bias_keys(5)
+        interleave("scalar", 9, 0, (5, 0))
+        interleave("vector", 9, 1, (8, 0))
+        bias_keys(6)
+        quantise(8, 1)
+        multiply_keys(8)
+        quantise(9, 0)
+        interleave("scalar", 10, 0, (5, 1))
+        bias_keys(7)
         bias_keys(8)
-        interleave("scalar", 11, 0)
+        interleave("vector", 10, 1, (9, 0))
+        quantise(9, 1)
+        multiply_keys(9)
+        quantise(10, 0)
+        interleave("scalar", 11, 0, (6, 1))
         bias_keys(9)
+        quantise(10, 1)
+        multiply_keys(10)
         interleave("vector", 11, 1, (10, 1), slice(0, 1))
-        interleave("scalar", 11, 1, (10, 1), slice(1, 2))
-        quantise(11, 0)
+        quantise(11, 0, slice(0, 1))
         quantise(11, 1, slice(0, 1))
         multiply_keys(11, [0])
+        bias_keys(10)
+        interleave("vector", 11, 1, (10, 1), slice(1, 2))
+        quantise(11, 0, slice(1, 2))
         quantise(11, 1, slice(1, 2))
         multiply_keys(11, [1])
-        bias_keys(10, [0])
-        bias_keys(11, [0])
-        bias_keys(10, [1])
-        bias_keys(11, [1])
-        fetch(2, 0, (5, 1))
-        fetch(2, 1, (6, 0))
-        fetch(2, 2, (6, 1))
+        bias_keys(11)
+        fetch(2, 0, (3, 0))
+        fetch(2, 1, (3, 1))
+        fetch(2, 2, (4, 0))
         accumulate(2, 1)
-        fetch(3, 0, (7, 0))
+        fetch(3, 0, (4, 1))
         accumulate(2, 2)
         fetch(3, 1, (7, 1))
         token_halves = [slice(0, T // 2), slice(T // 2, T)]
-        fetch(3, 2, (9, 0), token_halves[0])
+        fetch(3, 2, ("product", 2, 1), token_halves[0])
         accumulate(3, 1)
-        fetch(3, 2, (9, 0), token_halves[1])
+        fetch(3, 2, ("product", 2, 1), token_halves[1])
         accumulate(3, 2, token_halves[0])
         accumulate(3, 2, token_halves[1])

@@ -42,7 +42,7 @@ def tile_moe_qkv_kernel(
         xw = [keep.tile([P, T], I32, name=f"xw{s}", align_bytes=64) for s in range(PASSES)]
         xs = keep.tile([P, T], U8, name="xs", align_bytes=64)
         slot_words = keep.tile([P, PASSES, S], U32, name="slot_words", align_bytes=64)
-        slot_scales = [keep.tile([P, S], U8, name=f"slot_scales{s}", align_bytes=64) for s in range(PASSES)]
+        slot_scales = [keep.tile([P, S], U8, name="slot_scales0", align_bytes=64)]
         packed_words = [
             keep.tile([P, E * PASSES, 2 * N], U8, name=f"packed_words{i}", tag=f"words{i}", align_bytes=64) for i in range(2)
         ]
@@ -56,13 +56,15 @@ def tile_moe_qkv_kernel(
 
         nc.vector.memset(xs[:].bitcast(I32), 0)
         nc.vector.memset(packed_scales[0][:].rearrange("p a n -> p (a n)").bitcast(I32), 0)
-        nc.vector.memset(slot_scales[1][:].bitcast(I32), 0)
         nc.vector.memset(packed_scales[1][:].rearrange("p a n -> p (a n)").bitcast(I32), 0)
 
         raw = {}
 
         def load_wk(e, s):
-            raw[e, s] = raw_pool.tile([P, PACK, N], F32, name="raw")
+            if (e, s) == (0, 0):
+                raw[e, s] = keep.tile([P, PACK, N], F32, name="first_rows", tag="first_rows", align_bytes=64)
+            else:
+                raw[e, s] = raw_pool.tile([P, PACK, N], F32, name="raw")
             rows = wk[e, s * P * PACK : (s + 1) * P * PACK, :]
             nc.sync.dma_start(out=raw[e, s][:], in_=rows.rearrange("(p d) n -> p d n", d=PACK))
 
@@ -134,7 +136,7 @@ def tile_moe_qkv_kernel(
         load_wk(6, 1)
         load_wk(7, 0)
         load_wk(7, 1)
-        load_key_bias(3, 11)
+        load_key_bias(3, 8)
         load_wk(8, 0)
         load_wk(8, 1)
         load_wk(9, 0)
@@ -142,6 +144,7 @@ def tile_moe_qkv_kernel(
         load_wk(10, 0)
         load_wk(10, 1)
         load_wk(11, 0)
+        load_key_bias(8, 11)
         load_wk(11, 1)
 
         def chunk(c):
@@ -154,7 +157,9 @@ def tile_moe_qkv_kernel(
                 nc.vector.tensor_copy(slot_scales[0][:, slots], xs[:].indirect(entries))
 
         def move_scales():
-            nc.gpsimd.dma_start(out=slot_scales[1][0:112, :].bitcast(I32), in_=slot_scales[0][4:116, :].bitcast(I32))
+            slot_scales.append(keep.tile([P, S], U8, name="slot_scales1", tag="first_rows", align_bytes=64))
+            nc.scalar.dma_start(out=slot_scales[1][0:112, :].bitcast(I32), in_=slot_scales[0][4:116, :].bitcast(I32))
+            nc.scalar.dma_start(out=slot_scales[1][112:P, :].bitcast(I32), in_=slot_scales[0][112:P, :].bitcast(I32))
 
         def gather_words(c):
             slots, entries = chunk(c)
@@ -281,98 +286,110 @@ def tile_moe_qkv_kernel(
         quantise(1, 1)
         project_all_packed(0)
         step_back(4)
-        after_queries = reuse("words0", 6)
-        fresh.extend(after_queries[:2])
-        for b in range(4):
-            slot_of["spare", b] = after_queries[2 + b]
-        for e in (0, 1):
-            multiply_keys(e)
-            bias_keys(e)
+        spare = fresh[:]
+        fresh.clear()
+        after_queries = reuse("words0", 6) + reuse("scales0", 3)
+        fresh.extend(after_queries[: 2])
+        spare.extend(after_queries[2 :])
+        for b, slot in enumerate(spare):
+            slot_of["spare", b] = slot
+        multiply_keys(0)
+        bias_keys(0)
+        multiply_keys(1)
+        bias_keys(1)
         scalar_expert(2)
         fetch(0, 0, (0, 0))
         fetch(0, 1, (0, 1))
-        fetch(0, 2, (1, 0))
+        fetch(0, 2, ("spare", 0))
         accumulate(0, 1)
-        fetch(1, 0, (1, 1))
+        fetch(1, 0, ("spare", 1))
         accumulate(0, 2)
         fetch(1, 1, ("product", 0, 1))
-        quantise(2, 0)
-        fetch(1, 2, (2, 0))
-        quantise(2, 1)
+        fetch(1, 2, ("product", 0, 2))
         accumulate(1, 1)
+        quantise(2, 0)
+        quantise(2, 1)
         project_all_packed(1)
         step_back(2)
         fresh.extend(reuse("words1", 6) + reuse("scales1", 3))
-        scalar_expert(3)
+        interleave("scalar", 3, 0)
         multiply_keys(2)
+        bias_keys(2)
         fetch(4, 0, (2, 1))
         accumulate(1, 2)
-        fetch(4, 1, ("product", 0, 2))
-        interleave("scalar", 4, 0)
-        bias_keys(2)
-        interleave("scalar", 4, 1)
-        fetch(4, 2, ("spare", 0))
+        fetch(4, 1, ("spare", 2))
+        fetch(4, 2, ("spare", 3))
         accumulate(4, 1)
-        fetch(5, 0, ("spare", 1))
+        fetch(5, 0, ("spare", 4))
         accumulate(4, 2)
-        fetch(5, 1, ("spare", 2))
-        fetch(5, 2, ("spare", 3))
+        fetch(5, 1, ("product", 1, 1))
+        fetch(5, 2, ("product", 1, 2))
         accumulate(5, 1)
+        interleave("scalar", 3, 1)
         quantise(3, 0)
         accumulate(5, 2)
-        scalar_expert(5)
-        scalar_expert(6)
-        interleave("scalar", 7, 0)
-        interleave("scalar", 7, 1, ("product", 4, 1))
         quantise(3, 1)
         multiply_keys(3)
-        for e in (4, 5, 6):
-            quantise(e, 0)
-            quantise(e, 1)
-            multiply_keys(e)
-        interleave("vector", 8, 0, (6, 0))
-        quantise(7, 0)
-        interleave("vector", 8, 1, (7, 0))
+        interleave("scalar", 4, 0)
+        interleave("scalar", 4, 1)
+        quantise(4, 0)
+        quantise(4, 1)
+        multiply_keys(4)
+        interleave("scalar", 5, 0)
+        interleave("scalar", 5, 1)
+        quantise(5, 0)
+        quantise(5, 1)
+        multiply_keys(5)
+        interleave("scalar", 6, 0)
+        interleave("scalar", 6, 1)
+        quantise(6, 0)
+        quantise(6, 1)
+        multiply_keys(6)
+        interleave("scalar", 7, 0)
+        interleave("scalar", 7, 1, ("product", 4, 1))
         bias_keys(3)
         bias_keys(4)
+        bias_keys(5)
+        bias_keys(6)
+        quantise(7, 0)
         quantise(7, 1)
         multiply_keys(7)
+        interleave("vector", 8, 0, ("product", 5, 1))
+        interleave("vector", 8, 1, ("product", 5, 2))
         quantise(8, 0)
-        bias_keys(5)
-        interleave("scalar", 9, 0, (5, 0))
-        interleave("vector", 9, 1, (8, 0))
-        bias_keys(6)
         quantise(8, 1)
         multiply_keys(8)
-        quantise(9, 0)
-        interleave("scalar", 10, 0, (5, 1))
+        interleave("scalar", 9, 0, ("product", 4, 2))
+        interleave("vector", 9, 1, (8, 0))
         bias_keys(7)
-        bias_keys(8)
-        interleave("vector", 10, 1, (9, 0))
+        quantise(9, 0)
         quantise(9, 1)
         multiply_keys(9)
+        interleave("scalar", 10, 0, (3, 0))
+        interleave("vector", 10, 1, (8, 1))
         quantise(10, 0)
-        interleave("scalar", 11, 0, (6, 1))
-        bias_keys(9)
         quantise(10, 1)
         multiply_keys(10)
-        interleave("vector", 11, 1, (10, 1), slice(0, 1))
+        interleave("scalar", 11, 0, (3, 1))
+        bias_keys(8)
+        bias_keys(9)
+        bias_keys(10)
+        interleave("vector", 11, 1, (9, 1), slice(0, 1))
         quantise(11, 0, slice(0, 1))
         quantise(11, 1, slice(0, 1))
         multiply_keys(11, [0])
-        bias_keys(10)
-        interleave("vector", 11, 1, (10, 1), slice(1, 2))
+        interleave("scalar", 11, 1, (9, 1), slice(1, 2))
         quantise(11, 0, slice(1, 2))
         quantise(11, 1, slice(1, 2))
         multiply_keys(11, [1])
         bias_keys(11)
-        fetch(2, 0, (3, 0))
-        fetch(2, 1, (3, 1))
-        fetch(2, 2, (4, 0))
+        fetch(2, 0, (5, 1))
+        fetch(2, 1, (6, 0))
+        fetch(2, 2, (6, 1))
         accumulate(2, 1)
-        fetch(3, 0, (4, 1))
+        fetch(3, 0, (7, 0))
         accumulate(2, 2)
-        fetch(3, 1, (7, 1))
+        fetch(3, 1, (9, 0))
         token_halves = [slice(0, T // 2), slice(T // 2, T)]
         fetch(3, 2, ("product", 2, 1), token_halves[0])
         accumulate(3, 1)

@@ -1,6 +1,7 @@
 from contextlib import ExitStack
 
 import concourse.mybir as mybir
+from concourse.masks import make_identity
 
 K, T, E, C, N, TOP = 1024, 512, 12, 128, 256, 3
 FLOPS = 2 * E * C * K * 3 * N
@@ -25,6 +26,7 @@ HALVES = N // P
 CHUNK = 3
 LIST_ROWS = 16
 SLOTS = 4
+BLOCKS = T // P
 
 
 def tile_moe_qkv_kernel(
@@ -55,6 +57,9 @@ def tile_moe_qkv_kernel(
         work = keep.tile([P, SLOTS, T], F32, name="work", align_bytes=64)
 
         nc.vector.memset(xs[:].bitcast(I32), 0)
+        gate_rows = keep.tile([P, P], F32, name="gate_rows")
+        nc.vector.memset(gate_rows[:], 0.0)
+        nc.scalar.dma_start(out=gate_rows[: TOP * BLOCKS, :], in_=gate[:, 0, :].rearrange("r (b n) -> r b n", n=P))
         nc.vector.memset(packed_scales[0][:].rearrange("p a n -> p (a n)").bitcast(I32), 0)
         nc.vector.memset(packed_scales[1][:].rearrange("p a n -> p (a n)").bitcast(I32), 0)
 
@@ -114,11 +119,8 @@ def tile_moe_qkv_kernel(
         load_packed_words(0, wq_words, 6, 9)
         load_packed_words(0, wq_words, 9, 12)
         nc.sync.dma_start(pos_t[0][:], pos1)
-        nc.sync.dma_start(out=gate_t[:, 0, :], in_=gate[0])
         nc.sync.dma_start(pos_t[1][:], pos2)
-        nc.sync.dma_start(out=gate_t[:, 1, :], in_=gate[1])
         nc.sync.dma_start(pos_t[2][:], pos3)
-        nc.sync.dma_start(out=gate_t[:, 2, :], in_=gate[2])
         load_wk(2, 0)
         load_wk(2, 1)
         load_packed_scales(1, wv_scales)
@@ -166,17 +168,17 @@ def tile_moe_qkv_kernel(
             for s in range(PASSES):
                 nc.vector.tensor_copy(slot_words[:, s, slots], xw[s][:].bitcast(U32).indirect(entries))
 
-        banks = [psum.tile([P, C], F32, name=f"bank{b}") for b in range(8)]
+        banks = [psum.tile([P, T], F32, name=f"bank{b}") for b in range(8)]
         sums = {}
 
         def multiply(first_tile, e, h, operand, token_scales):
             slots = slice(e * C, (e + 1) * C)
             banks.append(banks.pop(0))
-            sums[first_tile + h, e] = banks[-1]
+            sums[first_tile + h, e] = banks[-1][:, :C]
             for s in range(PASSES):
                 codes, scales = operand(s, h)
                 nc.tensor.matmul_mx(
-                    out=sums[first_tile + h, e][:],
+                    out=sums[first_tile + h, e],
                     lhsT=codes,
                     lhsT_scale=scales,
                     rhs=slot_words[:, s, slots].bitcast(FP8X4),
@@ -191,7 +193,7 @@ def tile_moe_qkv_kernel(
 
         def add_bias(j, e):
             nc.scalar.activation(
-                out=y[j][:, e * C : (e + 1) * C], in_=sums[j, e][:], func=IDENTITY, bias=key_bias.get((j, e), bias_t[:, j, e : e + 1])
+                out=y[j][:, e * C : (e + 1) * C], in_=sums[j, e], func=IDENTITY, bias=key_bias.get((j, e), bias_t[:, j, e : e + 1])
             )
 
         def project_packed(i, e, halves):
@@ -272,6 +274,16 @@ def tile_moe_qkv_kernel(
             for s in range(PASSES):
                 interleave("scalar", e, s)
 
+        identity = keep.tile([P, P], F32, name="identity")
+        make_identity(nc, identity[:])
+        gate_cols = keep.tile([P, 16], F32, name="gate_cols")
+        nc.tensor.transpose(banks[TOP][:, :P], gate_rows[:], identity[:])
+        nc.scalar.copy(out=gate_cols[:], in_=banks[TOP][:, :16])
+        for r in range(TOP):
+            for b in range(BLOCKS):
+                column = gate_cols[:, r * BLOCKS + b : r * BLOCKS + b + 1]
+                nc.tensor.transpose(banks[r][:, b * P : (b + 1) * P], column.to_broadcast([P, P]), identity[:])
+            nc.scalar.copy(out=gate_t[:, r, :], in_=banks[r][:])
         scalar_expert(0)
         gather_scales()
         move_scales()

from contextlib import ExitStack

import concourse.mybir as mybir
from concourse.masks import make_identity

K, T, E, C, N, TOP = 1024, 512, 12, 128, 256, 3
FLOPS = 2 * E * C * K * 3 * N

F32 = mybir.dt.float32
BF16 = mybir.dt.bfloat16
I32 = mybir.dt.int32
U32 = mybir.dt.uint32
U16 = mybir.dt.uint16
U8 = mybir.dt.uint8
FP8X4 = mybir.dt.float8_e4m3fn_x4
FP4X4 = mybir.dt.float4_e2m1fn_x4
MULT = mybir.AluOpType.mult
ADD = mybir.AluOpType.add
IDENTITY = mybir.ActivationFunctionType.Identity

P = 128
PACK = 4
PASSES = K // (P * PACK)
S = E * C
HALVES = N // P
CHUNK = 3
LIST_ROWS = 16
SLOTS = 4
BLOCKS = T // P


def tile_moe_qkv_kernel(
    tc, x_words, x_scales, wq_words, wq_scales, wk, wv_words, wv_scales, bias, gate, offs, pos1, pos2, pos3, out
):
    nc = tc.nc
    with ExitStack() as ctx:
        keep = ctx.enter_context(tc.tile_pool(name="keep", bufs=1))
        raw_pool = ctx.enter_context(tc.tile_pool(name="raw", bufs=20))
        ring = ctx.enter_context(tc.tile_pool(name="ring", bufs=8))
        psum = ctx.enter_context(tc.psum_pool(name="psum", bufs=1))

        offs_t = keep.tile([P, S // LIST_ROWS], U16, name="offs_t")
        pos_t = [keep.tile([P, T // LIST_ROWS], U16, name=f"pos{r}_t") for r in range(TOP)]
        xw = [keep.tile([P, T], I32, name=f"xw{s}", align_bytes=64) for s in range(PASSES)]
        xs = keep.tile([P, T], U8, name="xs", align_bytes=64)
        slot_words = keep.tile([P, PASSES, S], U32, name="slot_words", align_bytes=64)
        slot_scales = [keep.tile([P, S], U8, name="slot_scales0", align_bytes=64)]
        packed_words = [
            keep.tile([P, E * PASSES, 2 * N], U8, name=f"packed_words{i}", tag=f"words{i}", align_bytes=64) for i in range(2)
        ]
        packed_scales = [
            keep.tile([P, E * PASSES, N], U8, name=f"packed_scales{i}", tag=f"scales{i}", align_bytes=64) for i in range(2)
        ]
        bias_t = keep.tile([P, 3 * HALVES, 16], F32, name="bias_t")
        gate_t = keep.tile([P, TOP, T], F32, name="gate_t")
        y = [keep.tile([P, S], F32, name=f"y{j}") for j in range(3 * HALVES)]
        work = keep.tile([P, SLOTS, T], F32, name="work", align_bytes=64)

        nc.vector.memset(xs[:].bitcast(I32), 0)
        gate_rows = keep.tile([P, P], F32, name="gate_rows")
        nc.vector.memset(gate_rows[:], 0.0)
        nc.scalar.dma_start(out=gate_rows[: TOP * BLOCKS, :], in_=gate[:, 0, :].rearrange("r (b n) -> r b n", n=P))
        nc.vector.memset(packed_scales[0][:].rearrange("p a n -> p (a n)").bitcast(I32), 0)
        nc.vector.memset(packed_scales[1][:].rearrange("p a n -> p (a n)").bitcast(I32), 0)

        raw = {}

        def load_wk(e, s):
            if (e, s) == (0, 0):
                raw[e, s] = keep.tile([P, PACK, N], F32, name="first_rows", tag="first_rows", align_bytes=64)
            else:
                raw[e, s] = raw_pool.tile([P, PACK, N], F32, name="raw")
            rows = wk[e, s * P * PACK : (s + 1) * P * PACK, :]
            nc.sync.dma_start(out=raw[e, s][:], in_=rows.rearrange("(p d) n -> p d n", d=PACK))

        def load_packed_words(i, words, e0, e1):
            nc.sync.dma_start(
                out=packed_words[i][:, e0 * PASSES : e1 * PASSES, :].bitcast(I32),
                in_=words[e0:e1].rearrange("e s p b -> p (e s) b").bitcast(I32),
            )

        def load_packed_scales(i, scales):
            for r in range(4):
                nc.sync.dma_start(
                    out=packed_scales[i][r:P:32, :, :].bitcast(I32),
                    in_=scales[:, :, r:16:4, :].rearrange("e s q n -> q (e s) n").bitcast(I32),
                )

        key_bias = {}

        def load_key_bias(e0, e1):
            later = keep.tile([P, HALVES, 8], F32, name=f"key_bias{e0}")
            nc.sync.dma_start(
                out=later[:, :, : e1 - e0], in_=bias[N : 2 * N, e0:e1].rearrange("(h p) e -> p h e", p=P)
            )
            for e in range(e0, e1):
                for h in range(HALVES):
                    key_bias[HALVES + h, e] = later[:, h, e - e0 : e - e0 + 1]

        def load_x_words(s):
            nc.sync.dma_start(out=xw[s][:], in_=x_words[s].rearrange("p t d -> p (t d)").bitcast(I32))

        nc.sync.dma_start(offs_t[:], offs)
        for q in range(4):
            nc.sync.dma_start(
                out=xs[32 * q : 32 * q + 4 * PASSES, :].bitcast(I32),
                in_=x_scales[:, 4 * q : 4 * q + 4, :].bitcast(I32),
            )
        load_x_words(0)
        load_x_words(1)
        load_wk(0, 0)
        load_wk(0, 1)
        nc.sync.dma_start(out=bias_t[:, :, :E], in_=bias.rearrange("(j p) e -> p j e", p=P))
        load_wk(1, 0)
        load_wk(1, 1)
        load_packed_scales(0, wq_scales)
        load_packed_words(0, wq_words, 0, 3)
        load_packed_words(0, wq_words, 3, 6)
        load_packed_words(0, wq_words, 6, 9)
        load_packed_words(0, wq_words, 9, 12)
        nc.sync.dma_start(pos_t[0][:], pos1)
        nc.sync.dma_start(pos_t[1][:], pos2)
        nc.sync.dma_start(pos_t[2][:], pos3)
        load_wk(2, 0)
        load_wk(2, 1)
        load_packed_scales(1, wv_scales)
        load_packed_words(1, wv_words, 0, 3)
        load_packed_words(1, wv_words, 3, 6)
        load_packed_words(1, wv_words, 6, 9)
        load_packed_words(1, wv_words, 9, 12)
        load_wk(3, 0)
        load_wk(3, 1)
        load_wk(4, 0)
        load_wk(4, 1)
        load_wk(5, 0)
        load_wk(5, 1)
        load_wk(6, 0)
        load_wk(6, 1)
        load_wk(7, 0)
        load_wk(7, 1)
        load_key_bias(3, 8)
        load_wk(8, 0)
        load_wk(8, 1)
        load_wk(9, 0)
        load_wk(9, 1)
        load_wk(10, 0)
        load_wk(10, 1)
        load_wk(11, 0)
        load_key_bias(8, 11)
        load_wk(11, 1)

        def chunk(c):
            slots = slice(c * CHUNK * C, (c + 1) * CHUNK * C)
            return slots, offs_t[:, slots.start // LIST_ROWS : slots.stop // LIST_ROWS]

        def gather_scales():
            for c in range(E // CHUNK):
                slots, entries = chunk(c)
                nc.vector.tensor_copy(slot_scales[0][:, slots], xs[:].indirect(entries))

        def move_scales():
            slot_scales.append(keep.tile([P, S], U8, name="slot_scales1", tag="first_rows", align_bytes=64))
            nc.scalar.dma_start(out=slot_scales[1][0:112, :].bitcast(I32), in_=slot_scales[0][4:116, :].bitcast(I32))
            nc.scalar.dma_start(out=slot_scales[1][112:P, :].bitcast(I32), in_=slot_scales[0][112:P, :].bitcast(I32))

        def gather_words(c):
            slots, entries = chunk(c)
            for s in range(PASSES):
                nc.vector.tensor_copy(slot_words[:, s, slots], xw[s][:].bitcast(U32).indirect(entries))

        banks = [psum.tile([P, T], F32, name=f"bank{b}") for b in range(8)]
        sums = {}

        def multiply(first_tile, e, h, operand, token_scales):
            slots = slice(e * C, (e + 1) * C)
            banks.append(banks.pop(0))
            sums[first_tile + h, e] = banks[-1][:, :C]
            for s in range(PASSES):
                codes, scales = operand(s, h)
                nc.tensor.matmul_mx(
                    out=sums[first_tile + h, e],
                    lhsT=codes,
                    lhsT_scale=scales,
                    rhs=slot_words[:, s, slots].bitcast(FP8X4),
                    rhs_scale=token_scales[s][:, slots],
                    start=(s == 0),
                    stop=(s == PASSES - 1),
                )

        def step_back(count):
            for turn in range(count):
                banks.insert(0, banks.pop())

        def add_bias(j, e):
            nc.scalar.activation(
                out=y[j][:, e * C : (e + 1) * C], in_=sums[j, e], func=IDENTITY, bias=key_bias.get((j, e), bias_t[:, j, e : e + 1])
            )

        def project_packed(i, e, halves):
            def operand(s, h):
                a = e * PASSES + s
                return (
                    packed_words[i][:, a, 2 * P * h : 2 * P * (h + 1)].bitcast(FP4X4),
                    packed_scales[i][:, a, P * h : P * (h + 1)],
                )

            for h in halves:
                multiply(2 * HALVES * i, e, h, operand, slot_scales)
                add_bias(2 * HALVES * i + h, e)

        def project_all_packed(i):
            for e in range(9):
                project_packed(i, e, range(HALVES))
            for h in range(HALVES):
                for e in range(9, E):
                    project_packed(i, e, [h])

        slot_of = {}
        fresh = [work[:, b, :] for b in range(SLOTS)]

        def reuse(tag, count):
            later = keep.tile([P, count, T], F32, name=f"after_{tag}", tag=tag, align_bytes=64)
            return [later[:, b, :] for b in range(count)]

        def interleave(engine, e, s, after=None, halves=slice(0, HALVES)):
            if (e, s) not in slot_of:
                slot_of[e, s] = fresh.pop(0) if after is None else slot_of[after]
            dst = slot_of[e, s].bitcast(BF16).rearrange("p (c i d) -> p c d i", i=4, d=PACK)
            src = raw[e, s][:].rearrange("p d (c i) -> p c d i", i=4)
            cols = slice(halves.start * P // 4, halves.stop * P // 4)
            if engine == "vector":
                nc.vector.tensor_copy(out=dst[:, cols], in_=src[:, cols])
            else:
                nc.scalar.copy(out=dst[:, cols], in_=src[:, cols])

        quantised = {}

        def quantise(e, s, halves=slice(0, HALVES)):
            if (e, s) not in quantised:
                codes = ring.tile([P, N], U32, name="key_codes", align_bytes=64)
                scales = ring.tile([P, N], U8, name="key_scales", align_bytes=64)
                quantised[e, s] = (codes, scales)
            codes, scales = quantised[e, s]
            cols = slice(halves.start * P, halves.stop * P)
            grouped = slot_of[e, s].bitcast(BF16)
            nc.vector.quantize_mx(
                out=codes[:, cols].bitcast(FP8X4), scales=scales[:, cols], in_=grouped[:, cols.start * PACK : cols.stop * PACK]
            )

        def multiply_keys(e, halves=range(HALVES)):
            def operand(s, h):
                codes, scales = quantised[e, s]
                return codes[:, P * h : P * (h + 1)].bitcast(FP8X4), scales[:, P * h : P * (h + 1)]

            for h in halves:
                multiply(HALVES, e, h, operand, [slot_scales[0][:, :], slot_scales[0][4:P, :]])

        def bias_keys(e, halves=range(HALVES)):
            for h in halves:
                add_bias(HALVES + h, e)

        def fetch(j, r, after, cols=slice(0, T)):
            slot_of["product", j, r] = slot_of[after]
            entries = pos_t[r][:, cols.start // LIST_ROWS : cols.stop // LIST_ROWS]
            nc.vector.tensor_tensor(slot_of[after][:, cols], y[j][:].indirect(entries), gate_t[:, r, cols], MULT)

        def accumulate(j, r, cols=slice(0, T)):
            total = slot_of["product", j, 0][:, cols]
            nc.vector.tensor_tensor(total, total, slot_of["product", j, r][:, cols], ADD)
            if r == TOP - 1:
                nc.sync.dma_start(out=out[j * P : (j + 1) * P, cols], in_=total)

        def scalar_expert(e):
            for s in range(PASSES):
                interleave("scalar", e, s)

        identity = keep.tile([P, P], F32, name="identity")
        make_identity(nc, identity[:])
        gate_cols = keep.tile([P, 16], F32, name="gate_cols")
        nc.tensor.transpose(banks[TOP][:, :P], gate_rows[:], identity[:])
        nc.scalar.copy(out=gate_cols[:], in_=banks[TOP][:, :16])
        for r in range(TOP):
            for b in range(BLOCKS):
                column = gate_cols[:, r * BLOCKS + b : r * BLOCKS + b + 1]
                nc.tensor.transpose(banks[r][:, b * P : (b + 1) * P], column.to_broadcast([P, P]), identity[:])
            nc.scalar.copy(out=gate_t[:, r, :], in_=banks[r][:])
        scalar_expert(0)
        gather_scales()
        move_scales()
        gather_words(0)
        scalar_expert(1)
        gather_words(1)
        gather_words(2)
        gather_words(3)
        quantise(0, 0)
        quantise(0, 1)
        quantise(1, 0)
        quantise(1, 1)
        project_all_packed(0)
        step_back(4)
        spare = fresh[:]
        fresh.clear()
        after_queries = reuse("words0", 6) + reuse("scales0", 3)
        fresh.extend(after_queries[: 2])
        spare.extend(after_queries[2 :])
        for b, slot in enumerate(spare):
            slot_of["spare", b] = slot
        multiply_keys(0)
        bias_keys(0)
        multiply_keys(1)
        bias_keys(1)
        scalar_expert(2)
        fetch(0, 0, (0, 0))
        fetch(0, 1, (0, 1))
        fetch(0, 2, ("spare", 0))
        accumulate(0, 1)
        fetch(1, 0, ("spare", 1))
        accumulate(0, 2)
        fetch(1, 1, ("product", 0, 1))
        fetch(1, 2, ("product", 0, 2))
        accumulate(1, 1)
        quantise(2, 0)
        quantise(2, 1)
        project_all_packed(1)
        step_back(2)
        fresh.extend(reuse("words1", 6) + reuse("scales1", 3))
        interleave("scalar", 3, 0)
        multiply_keys(2)
        bias_keys(2)
        fetch(4, 0, (2, 1))
        accumulate(1, 2)
        fetch(4, 1, ("spare", 2))
        fetch(4, 2, ("spare", 3))
        accumulate(4, 1)
        fetch(5, 0, ("spare", 4))
        accumulate(4, 2)
        fetch(5, 1, ("product", 1, 1))
        fetch(5, 2, ("product", 1, 2))
        accumulate(5, 1)
        interleave("scalar", 3, 1)
        quantise(3, 0)
        accumulate(5, 2)
        quantise(3, 1)
        multiply_keys(3)
        interleave("scalar", 4, 0)
        interleave("scalar", 4, 1)
        quantise(4, 0)
        quantise(4, 1)
        multiply_keys(4)
        interleave("scalar", 5, 0)
        interleave("scalar", 5, 1)
        quantise(5, 0)
        quantise(5, 1)
        multiply_keys(5)
        interleave("scalar", 6, 0)
        interleave("scalar", 6, 1)
        quantise(6, 0)
        quantise(6, 1)
        multiply_keys(6)
        interleave("scalar", 7, 0)
        interleave("scalar", 7, 1, ("product", 4, 1))
        bias_keys(3)
        bias_keys(4)
        bias_keys(5)
        bias_keys(6)
        quantise(7, 0)
        quantise(7, 1)
        multiply_keys(7)
        interleave("vector", 8, 0, ("product", 5, 1))
        interleave("vector", 8, 1, ("product", 5, 2))
        quantise(8, 0)
        quantise(8, 1)
        multiply_keys(8)
        interleave("scalar", 9, 0, ("product", 4, 2))
        interleave("vector", 9, 1, (8, 0))
        bias_keys(7)
        quantise(9, 0)
        quantise(9, 1)
        multiply_keys(9)
        interleave("scalar", 10, 0, (3, 0))
        interleave("vector", 10, 1, (8, 1))
        quantise(10, 0)
        quantise(10, 1)
        multiply_keys(10)
        interleave("scalar", 11, 0, (3, 1))
        bias_keys(8)
        bias_keys(9)
        bias_keys(10)
        interleave("vector", 11, 1, (9, 1), slice(0, 1))
        quantise(11, 0, slice(0, 1))
        quantise(11, 1, slice(0, 1))
        multiply_keys(11, [0])
        interleave("scalar", 11, 1, (9, 1), slice(1, 2))
        quantise(11, 0, slice(1, 2))
        quantise(11, 1, slice(1, 2))
        multiply_keys(11, [1])
        bias_keys(11)
        fetch(2, 0, (5, 1))
        fetch(2, 1, (6, 0))
        fetch(2, 2, (6, 1))
        accumulate(2, 1)
        fetch(3, 0, (7, 0))
        accumulate(2, 2)
        fetch(3, 1, (9, 0))
        token_halves = [slice(0, T // 2), slice(T // 2, T)]
        fetch(3, 2, ("product", 2, 1), token_halves[0])
        accumulate(3, 1)
        fetch(3, 2, ("product", 2, 1), token_halves[1])
        accumulate(3, 2, token_halves[0])
        accumulate(3, 2, token_halves[1])
